import numpy as np
import ml_dtypes


def mxq(x, axis, fmt="e4m3"):
    dtype, down = {"e4m3": (ml_dtypes.float8_e4m3fn, 7), "e5m2": (ml_dtypes.float8_e5m2, 14)}[fmt]
    v = np.moveaxis(np.asarray(x, np.float32).astype(ml_dtypes.bfloat16).astype(np.float64), axis, -1)
    blocks = v.reshape(v.shape[:-1] + (-1, 32))
    amax = np.abs(blocks).max(-1, keepdims=True)
    byte = np.maximum(np.where(amax > 0, np.frexp(amax)[1] - 1 + 127, 0) - down, 1)
    scale = np.exp2(byte - 127.0)
    codes = (blocks / scale).astype(np.float32).astype(dtype).astype(np.float64)
    return np.moveaxis((codes * scale).reshape(v.shape), -1, axis)


WIDE = False


def mx_kscale(k):
    if not WIDE:
        return np.ones(k)
    levels = np.array([10, -10, 5, -5, 0])
    if k % 512:
        return np.exp2(np.random.permutation(np.resize(levels, k // 32))).repeat(32)
    a = np.empty((k // 512, 16))
    for p in range(k // 512):
        a[p, :8] = np.random.permutation(np.resize(levels, 8))
        for g in range(8):
            far = levels[np.abs(levels - a[p, g]) >= 10]
            a[p, g + 8] = far[np.random.randint(len(far))]
    return np.exp2(a.ravel()).repeat(32)


def f64(x):
    return np.asarray(x).astype(np.float64)


def striped(idx):
    return np.tile(idx.reshape(-1, 16).T, (8, 1)).astype(np.uint16)


def unstriped(offs):
    return offs[:16].T.reshape(-1).astype(np.int64)


def striped8(idx):
    return np.concatenate([x.reshape(-1, 16).T for x in idx]).astype(np.uint16)


def runs(offs, k):
    lists = np.stack([offs[16 * r : 16 * r + 16].T.reshape(-1) for r in range(8)]).astype(np.int64)
    return lists[np.arange(k) % 512 // 64]


def pack_weight(w):
    k, n = w.shape
    w = f64(np.asarray(w, np.float32).astype(ml_dtypes.bfloat16)).reshape(k // 32, 32, n)
    amax = np.abs(w).max(1)
    byte = np.clip(np.where(amax > 0, np.frexp(amax)[1] - 1 + 127 - 7, 1), 1, 254)
    scaled = (w * np.exp2(127.0 - byte)[:, None, :]).reshape(k, n).astype(np.float32)
    words = np.ascontiguousarray(scaled.reshape(k // 512, 128, 4, n).transpose(0, 1, 3, 2)).astype(ml_dtypes.float8_e4m3fn).view(np.uint8)
    return words, np.ascontiguousarray(byte.astype(np.uint8).reshape(k // 512, 16, n))


def unpack_weight(words, scales):
    g, p, n, _ = words.shape
    vals = np.ascontiguousarray(words).view(ml_dtypes.float8_e4m3fn).astype(np.float64) * np.repeat(np.exp2(scales.astype(np.float64) - 127.0), 8, axis=1)[..., None]
    return vals.transpose(0, 1, 3, 2).reshape(g * 512, n)


def sigmoid(v):
    return 1.0 / (1.0 + np.exp(-np.maximum(v, -700.0)))


K, T, S, N, G, H, W, U = 512, 1024, 256, 512, 2048, 512, 128, 512


def setup_inputs():
    n = np.random.standard_normal
    s = mx_kscale(K)[:, None]
    u = mx_kscale(K)
    packed_xT = pack_weight(n((K, T)) * s)
    packed_dT = pack_weight(n((K, G)) / s)
    perm = np.random.permutation(S)
    perm2 = np.random.permutation(S)
    perm3 = np.random.permutation(U)
    return {
        "x_words": packed_xT[0],
        "x_scales": packed_xT[1],
        "d_words": packed_dT[0],
        "d_scales": packed_dT[1],
        "sl": np.random.uniform(1.0, 2.0, (H, 1)).astype(np.float32),
        "th": (0.5 * n((H, 1))).astype(np.float32),
        "gn": (np.random.uniform(0.5, 1.5, (H, 1)) * u[:, None]).astype(np.float32),
        "w1": (n((H, N)) / np.sqrt(2 * H) / u[:, None]).astype(np.float32),
        "w2": (n((K, N)) / np.sqrt(2 * K) / s).astype(np.float32),
        "offs": striped(np.random.permutation(T)[:S]),
        "ka": striped8(np.random.randint(0, G, (8, H))),
        "kb": striped8(np.random.randint(0, G, (8, H))),
        "n1": striped(perm[:W]),
        "n2": striped(perm[W:]),
        "n3": striped(perm2[:W]),
        "n4": striped(perm2[W:]),
        "n5": striped(np.random.permutation(S)),
        "hz": striped8(np.random.randint(0, T, (8, S))),
        "n6": striped(perm3[:S]),
        "n7": striped(perm3[S:]),
        "n8": striped(np.random.permutation(S)),
        "n9": striped(np.random.permutation(S)),
    }


def reference(x_words, x_scales, d_words, d_scales, sl, th, gn, w1, w2, offs, ka, kb, n1, n2, n3, n4, n5, hz, n6, n7, n8, n9):
    d_ka = unpack_weight(d_words, d_scales)[np.arange(K)[:, None], runs(ka, K)]
    xq = unpack_weight(x_words, x_scales)[:, unstriped(offs)]
    d_kb = unpack_weight(d_words, d_scales)[np.arange(K)[:, None], runs(kb, K)]
    h = 0.0625 * (d_ka.T @ xq + d_kb.T @ xq)
    pa = h[:, unstriped(n1)]
    pb = h[:, unstriped(n2)]
    rb = np.minimum(pa, pb)
    ra = np.maximum(pa, pb)
    ua = np.zeros((H, S))
    ua[:, unstriped(n3)] = ra
    ub = ua.copy()
    ub[:, unstriped(n4)] = rb
    sg = sigmoid(f64(sl) * (ub[:, unstriped(n5)] - f64(th)))
    z = f64(gn) * (ub * sg)
    x_hz = unpack_weight(x_words, x_scales)[np.arange(K)[:, None], runs(hz, K)]
    h2 = mxq(f64(w1), 0, "e4m3").T @ mxq(z, 0, "e4m3") + mxq(f64(w2), 0, "e4m3").T @ x_hz
    dn = h2 - h2[:, unstriped(n9)]
    up = np.maximum(h2, h2[:, unstriped(n8)])
    ph = np.zeros((N, U))
    ph[:, unstriped(n6)] = up
    out = ph.copy()
    out[:, unstriped(n7)] = dn
    return out

@@ -1,0 +1,273 @@
+from contextlib import ExitStack
+
+import concourse.mybir as mybir
+
+K, T, S, N, G, H, W, U = 512, 1024, 256, 512, 2048, 512, 128, 512
+FLOPS = 2 * (2 * K * H * S + H * N * S + K * N * S)
+
+F32 = mybir.dt.float32
+BF16 = mybir.dt.bfloat16
+I32 = mybir.dt.int32
+U32 = mybir.dt.uint32
+U16 = mybir.dt.uint16
+U8 = mybir.dt.uint8
+FP8X4 = mybir.dt.float8_e4m3fn_x4
+ALU = mybir.AluOpType
+ACT = mybir.ActivationFunctionType
+
+P = 128
+PACK = 4
+HALF = S // 2
+SPARE = 16
+
+
+def tile_picked_atznheordpagdd_none_p_kernel(
+    tc, x_words, x_scales, d_words, d_scales, sl, th, gn, w1, w2,
+    offs, ka, kb, n1, n2, n3, n4, n5, hz, n6, n7, n8, n9, out,
+):
+    nc = tc.nc
+    with ExitStack() as ctx:
+        lists = ctx.enter_context(tc.tile_pool(name="lists", bufs=1))
+        keep = ctx.enter_context(tc.tile_pool(name="keep", bufs=1))
+        psum = ctx.enter_context(tc.psum_pool(name="psum", bufs=1))
+
+        def load_list(src, name):
+            tile = lists.tile(list(src.shape), U16, name=name)
+            nc.sync.dma_start(tile[:], src)
+            return tile
+
+        def load_scales(src, width, name):
+            tile = keep.tile([P, width], U8, name=name, align_bytes=64)
+            rows = src[0].bitcast(I32).unsqueeze(1).broadcast_to([16, 8, width // 4])
+            nc.sync.dma_start(tile[:].bitcast(I32), rows)
+            return tile
+
+        def load_words(src, width, name):
+            tile = keep.tile([P, width], U32, name=name, tag=name, align_bytes=64)
+            nc.sync.dma_start(tile[:].bitcast(I32), src[0].rearrange("p n t -> p (n t)").bitcast(I32))
+            return tile
+
+        def load_column(src, name):
+            tile = keep.tile([P, PACK], F32, name=name)
+            nc.sync.dma_start(tile[:], src.rearrange("(p t) o -> p (t o)", t=PACK))
+            return tile
+
+        def place_scale_rows(queue, plane, picked):
+            for a in range(4):
+                queue.dma_start(plane[a:P:32, :].bitcast(I32), picked[8 * a:P:32, :].bitcast(I32))
+
+        offs_l = load_list(offs, "offs_l")
+        x_bytes = load_scales(x_scales, T, "x_bytes")
+        d_bytes = load_scales(d_scales, G, "d_bytes")
+        ka_l = load_list(ka, "ka_l")
+        kb_l = load_list(kb, "kb_l")
+        x_codes = load_words(x_words, T, "x_codes")
+        d_codes = load_words(d_words, G, "d_codes")
+
+        plane1 = keep.tile([P, 2 * H + S], U8, align_bytes=64)
+        nc.vector.memset(plane1[:].bitcast(I32), 0)
+        hz_plane = keep.tile([P, S], U8, align_bytes=64)
+        nc.vector.memset(hz_plane[:].bitcast(I32), 0)
+        h2 = [keep.tile([P, S + SPARE], F32, name=f"h2_{b}") for b in range(4)]
+        for b in range(4):
+            nc.vector.memset(h2[b][:, S:], 0.0)
+
+        picked1 = keep.tile([P, 2 * H + S], U8, tag="early", align_bytes=64)
+        nc.vector.tensor_copy(picked1[:, 2 * H:], x_bytes[:].indirect(offs_l[:]))
+        nc.vector.tensor_copy(picked1[:, 0:H], d_bytes[:].indirect(ka_l[:]))
+        nc.vector.tensor_copy(picked1[:, H:2 * H], d_bytes[:].indirect(kb_l[:]))
+        place_scale_rows(nc.scalar, plane1, picked1)
+
+        xq = keep.tile([P, S], U32, align_bytes=64)
+        nc.vector.tensor_copy(xq[:], x_codes[:].indirect(offs_l[:]))
+        dq = keep.tile([P, 2, H], U32, align_bytes=64)
+        nc.vector.tensor_copy(dq[:, 0, :], d_codes[:].indirect(ka_l[:]))
+        nc.vector.tensor_copy(dq[:, 1, :], d_codes[:].indirect(kb_l[:]))
+
+        def load_w(half, tag):
+            tile = keep.tile([P, 2, PACK, N // 2], F32, name=f"w_raw_{half}", tag=tag, align_bytes=64)
+            for i, src in ((1, w2), (0, w1)):
+                rows = src.rearrange("(p j) m -> p j m", j=PACK)
+                nc.sync.dma_start(tile[:, i], rows[:, :, half * 256:(half + 1) * 256])
+            return tile
+
+        n1_l = load_list(n1, "n1_l")
+        n2_l = load_list(n2, "n2_l")
+        n3_l = load_list(n3, "n3_l")
+        n4_l = load_list(n4, "n4_l")
+        hz_l = load_list(hz, "hz_l")
+        n5_l = load_list(n5, "n5_l")
+        sl_c = load_column(sl, "sl_c")
+        w_raw = [load_w(0, "early")]
+        th_c = load_column(th, "th_c")
+        gn_c = load_column(gn, "gn_c")
+        n8_l = load_list(n8, "n8_l")
+        n9_l = load_list(n9, "n9_l")
+        n6_l = load_list(n6, "n6_l")
+        n7_l = load_list(n7, "n7_l")
+        w_raw.append(load_w(1, "d_codes"))
+
+        bias = keep.tile([P, PACK], F32)
+        nc.vector.scalar_tensor_tensor(bias[:], sl_c[:], -1.0, th_c[:], ALU.mult, ALU.mult)
+
+        h = [keep.tile([P, S], F32, name=f"h_{t}", tag=f"h_{t}") for t in range(4)]
+        pab = [keep.tile([P, 2, W], F32, name=f"pab_{t}", tag=f"pab_{t}", align_bytes=64) for t in range(4)]
+        ra = [keep.tile([P, W], F32, name=f"ra_{t}") for t in range(4)]
+        ub = [keep.tile([P, S], F32, name=f"ub_{t}") for t in range(4)]
+        sg = [keep.tile([P, S], F32, name=f"sg_{t}") for t in range(4)]
+        z_rows = keep.tile([P, PACK, S], BF16, align_bytes=64)
+        h_acc = {}
+
+        def first_product(t):
+            codes = keep.tile([P, 2, P], U32, name=f"d_dealt_{t}", tag="d_dealt", bufs=2, align_bytes=64)
+            scales = keep.tile([P, 2, P], U8, name=f"d_dealt_s_{t}", align_bytes=64)
+            nc.vector.tensor_copy(
+                scales[:], plane1[:, 0:2 * H].rearrange("p (l m t) -> p l m t", l=2, t=PACK)[:, :, :, t]
+            )
+            nc.vector.tensor_copy(codes[:], dq[:].rearrange("p l (m t) -> p l m t", t=PACK)[:, :, :, t])
+            h_acc[t] = psum.tile([P, S], F32, name=f"h_acc_{t}", tag=f"bank_{t}")
+            for l in range(2):
+                nc.tensor.matmul_mx(
+                    out=h_acc[t][:], lhsT=codes[:, l, :].bitcast(FP8X4), lhsT_scale=scales[:, l, :],
+                    rhs=xq[:].bitcast(FP8X4), rhs_scale=plane1[:, 2 * H:], start=(l == 0), stop=(l == 1),
+                )
+
+        def fetch_pairs(t):
+            nc.vector.tensor_scalar(h[t][:], h_acc[t][:], 0.0625, None, ALU.mult)
+            nc.scalar.activation(pab[t][:, 0, :], h[t][:].indirect(n1_l[:]), ACT.Copy)
+            nc.scalar.activation(pab[t][:, 1, :], h[t][:].indirect(n2_l[:]), ACT.Copy)
+
+        def put_larger(t):
+            nc.vector.tensor_tensor(ra[t][:], pab[t][:, 0, :], pab[t][:, 1, :], ALU.max)
+            nc.scalar.activation(ub[t][:].indirect(n3_l[:]), ra[t][:], ACT.Copy)
+
+        def put_smaller(t):
+            rb = keep.tile([P, W], F32, name=f"rb_{t}", tag=f"h_{(t + 2) % 4}")
+            nc.vector.tensor_tensor(rb[:], pab[t][:, 0, :], pab[t][:, 1, :], ALU.min)
+            nc.scalar.activation(ub[t][:].indirect(n4_l[:]), rb[:], ACT.Copy)
+
+        def gate(t, c):
+            cols = slice(c * HALF, (c + 1) * HALF)
+            nc.scalar.activation(
+                sg[t][:, cols], ub[t][:].indirect(n5_l[:, c * 8:(c + 1) * 8]), ACT.Sigmoid,
+                bias=bias[:, t:t + 1], scale=sl_c[:, t:t + 1],
+            )
+            nc.vector.scalar_tensor_tensor(
+                z_rows[:, t, cols], ub[t][:, cols], gn_c[:, t:t + 1], sg[t][:, cols], ALU.mult, ALU.mult
+            )
+
+        z_codes = keep.tile([P, S], U32, align_bytes=64)
+        z_scales = keep.tile([P, S], U8, align_bytes=64)
+
+        def quantise_z(c):
+            cols = slice(c * HALF, (c + 1) * HALF)
+            grouped = keep.tile([P, HALF, PACK], BF16, name=f"z_grouped_{c}", align_bytes=64)
+            nc.vector.tensor_copy(
+                grouped[:].rearrange("p (c i) t -> p c t i", i=4),
+                z_rows[:, :, cols].rearrange("p t (c i) -> p c t i", i=4),
+            )
+            nc.vector.quantize_mx(
+                out=z_codes[:, cols].bitcast(FP8X4), scales=z_scales[:, cols],
+                in_=grouped[:].rearrange("p c t -> p (c t)"),
+            )
+
+        w_codes = [keep.tile([P, 2, P], U32, name=f"w_codes_{b}", align_bytes=64) for b in range(4)]
+        w_scales = [keep.tile([P, 2, P], U8, name=f"w_scales_{b}", align_bytes=64) for b in range(4)]
+        w_grouped = {}
+
+        def group_w(b, tag):
+            w_grouped[b] = keep.tile([P, 2, P, PACK], BF16, name=f"w_grouped_{b}", tag=tag, align_bytes=64)
+            for i in range(2):
+                nc.vector.tensor_copy(
+                    w_grouped[b][:, i].rearrange("p (c i) t -> p c t i", i=4),
+                    w_raw[b // 2][:, i, :, (b % 2) * P:(b % 2 + 1) * P].rearrange("p t (c i) -> p c t i", i=4),
+                )
+
+        def quantise_w(b):
+            nc.vector.quantize_mx(
+                out=w_codes[b][:].rearrange("p i m -> p (i m)").bitcast(FP8X4),
+                scales=w_scales[b][:].rearrange("p i m -> p (i m)"),
+                in_=w_grouped[b][:].rearrange("p i m t -> p (i m t)"),
+            )
+
+        first_product(0)
+        first_product(1)
+        fetch_pairs(0)
+        first_product(2)
+        fetch_pairs(1)
+        first_product(3)
+        put_larger(0)
+        fetch_pairs(2)
+        fetch_pairs(3)
+        put_larger(1)
+        put_larger(2)
+        put_smaller(0)
+        put_larger(3)
+        put_smaller(1)
+
+        put_smaller(2)
+        put_smaller(3)
+
+        picked_hz = keep.tile([P, S], U8, tag="pab_2", align_bytes=64)
+        nc.vector.tensor_copy(picked_hz[:], x_bytes[:].indirect(hz_l[:]))
+        place_scale_rows(nc.sync, hz_plane, picked_hz)
+        x_hz = keep.tile([P, S], U32, tag="pab_3", align_bytes=64)
+        nc.vector.tensor_copy(x_hz[:], x_codes[:].indirect(hz_l[:]))
+
+        group_w(0, "wg0")
+        group_w(1, "wg1")
+        quantise_w(0)
+        quantise_w(1)
+        for c in range(2):
+            for t in range(4):
+                gate(t, c)
+            quantise_z(c)
+
+        g89 = [keep.tile([P, 2, S], F32, name=f"g89_{b}", tag=f"g89_{b}", align_bytes=64) for b in range(4)]
+        updn = [keep.tile([P, 2, S], F32, name=f"updn_{b}") for b in range(4)]
+        page = [keep.tile([P, U], F32, name=f"page_{b}") for b in range(4)]
+
+        def second_product(b, c):
+            cols = slice(c * HALF, (c + 1) * HALF)
+            acc = psum.tile([P, HALF], F32, name=f"h2_acc_{b}_{c}", tag=f"bank_{4 * c + b}")
+            nc.tensor.matmul_mx(
+                out=acc[:], lhsT=w_codes[b][:, 1, :].bitcast(FP8X4), lhsT_scale=w_scales[b][:, 1, :],
+                rhs=x_hz[:, cols].bitcast(FP8X4), rhs_scale=hz_plane[:, cols], start=True, stop=False,
+            )
+            nc.tensor.matmul_mx(
+                out=acc[:], lhsT=w_codes[b][:, 0, :].bitcast(FP8X4), lhsT_scale=w_scales[b][:, 0, :],
+                rhs=z_codes[:, cols].bitcast(FP8X4), rhs_scale=z_scales[:, cols], start=False, stop=True,
+            )
+            nc.vector.tensor_copy(h2[b][:, cols], acc[:])
+
+        def fetch_neighbours(b):
+            nc.scalar.activation(g89[b][:, 0, :], h2[b][:].indirect(n8_l[:]), ACT.Copy)
+            nc.scalar.activation(g89[b][:, 1, :], h2[b][:].indirect(n9_l[:]), ACT.Copy)
+            nc.vector.tensor_tensor(updn[b][:, 0, :], h2[b][:, 0:S], g89[b][:, 0, :], ALU.max)
+            nc.vector.tensor_tensor(updn[b][:, 1, :], h2[b][:, 0:S], g89[b][:, 1, :], ALU.subtract)
+
+        def put_page(b):
+            nc.scalar.activation(page[b][:].indirect(n6_l[:]), updn[b][:, 0, :], ACT.Copy)
+            nc.scalar.activation(page[b][:].indirect(n7_l[:]), updn[b][:, 1, :], ACT.Copy)
+            nc.sync.dma_start(out[b * P:(b + 1) * P, :], page[b][:])
+
+        second_product(0, 0)
+        second_product(0, 1)
+        second_product(1, 0)
+        second_product(1, 1)
+        fetch_neighbours(0)
+        fetch_neighbours(1)
+        group_w(2, "g89_0")
+        quantise_w(2)
+        second_product(2, 0)
+        second_product(2, 1)
+        put_page(0)
+        group_w(3, "g89_1")
+        quantise_w(3)
+        second_product(3, 0)
+        second_product(3, 1)
+        fetch_neighbours(2)
+        put_page(1)
+        fetch_neighbours(3)
+        put_page(2)
+        put_page(3)

@@ -64,6 +64,10 @@ def tile_picked_atznheordpagdd_none_p_kernel(
         x_codes = load_words(x_words, T, "x_codes")
         d_codes = load_words(d_words, G, "d_codes")
 
+        warm = keep.tile([P, 16], F32)
+        nc.gpsimd.memset(warm[:, 0:1], 0.0)
+        nc.scalar.activation(warm[:, 8:9], warm[:, 0:1], ACT.Sigmoid)
+
         plane1 = keep.tile([P, 2 * H + S], U8, align_bytes=64)
         nc.vector.memset(plane1[:].bitcast(I32), 0)
         hz_plane = keep.tile([P, S], U8, align_bytes=64)

@@ -38,8 +38,8 @@ def tile_picked_atznheordpagdd_none_p_kernel(
 
         def load_scales(src, width, name):
             tile = keep.tile([P, width], U8, name=name, align_bytes=64)
-            rows = src[0].bitcast(I32).unsqueeze(1).broadcast_to([16, 8, width // 4])
-            nc.sync.dma_start(tile[:].bitcast(I32), rows)
+            nc.vector.memset(tile[:].bitcast(I32), 0)
+            nc.sync.dma_start(tile[0:P:8, :].bitcast(I32), src[0].bitcast(I32))
             return tile
 
         def load_words(src, width, name):
@@ -61,8 +61,8 @@ def tile_picked_atznheordpagdd_none_p_kernel(
         d_bytes = load_scales(d_scales, G, "d_bytes")
         ka_l = load_list(ka, "ka_l")
         kb_l = load_list(kb, "kb_l")
-        x_codes = load_words(x_words, T, "x_codes")
         d_codes = load_words(d_words, G, "d_codes")
+        x_codes = load_words(x_words, T, "x_codes")
 
         warm = keep.tile([P, 16], F32)
         nc.gpsimd.memset(warm[:, 0:1], 0.0)
@@ -82,11 +82,11 @@ def tile_picked_atznheordpagdd_none_p_kernel(
         nc.vector.tensor_copy(picked1[:, H:2 * H], d_bytes[:].indirect(kb_l[:]))
         place_scale_rows(nc.scalar, plane1, picked1)
 
-        xq = keep.tile([P, S], U32, align_bytes=64)
-        nc.vector.tensor_copy(xq[:], x_codes[:].indirect(offs_l[:]))
         dq = keep.tile([P, 2, H], U32, align_bytes=64)
         nc.vector.tensor_copy(dq[:, 0, :], d_codes[:].indirect(ka_l[:]))
         nc.vector.tensor_copy(dq[:, 1, :], d_codes[:].indirect(kb_l[:]))
+        xq = keep.tile([P, S], U32, align_bytes=64)
+        nc.vector.tensor_copy(xq[:], x_codes[:].indirect(offs_l[:]))
 
         def load_w(half, tag):
             tile = keep.tile([P, 2, PACK, N // 2], F32, name=f"w_raw_{half}", tag=tag, align_bytes=64)

from contextlib import ExitStack

import concourse.mybir as mybir

K, T, S, N, G, H, W, U = 512, 1024, 256, 512, 2048, 512, 128, 512
FLOPS = 2 * (2 * K * H * S + H * N * S + K * N * S)

F32 = mybir.dt.float32
BF16 = mybir.dt.bfloat16
I32 = mybir.dt.int32
U32 = mybir.dt.uint32
U16 = mybir.dt.uint16
U8 = mybir.dt.uint8
FP8X4 = mybir.dt.float8_e4m3fn_x4
ALU = mybir.AluOpType
ACT = mybir.ActivationFunctionType

P = 128
PACK = 4
HALF = S // 2
SPARE = 16


def tile_picked_atznheordpagdd_none_p_kernel(
    tc, x_words, x_scales, d_words, d_scales, sl, th, gn, w1, w2,
    offs, ka, kb, n1, n2, n3, n4, n5, hz, n6, n7, n8, n9, out,
):
    nc = tc.nc
    with ExitStack() as ctx:
        lists = ctx.enter_context(tc.tile_pool(name="lists", bufs=1))
        keep = ctx.enter_context(tc.tile_pool(name="keep", bufs=1))
        psum = ctx.enter_context(tc.psum_pool(name="psum", bufs=1))

        def load_list(src, name):
            tile = lists.tile(list(src.shape), U16, name=name)
            nc.sync.dma_start(tile[:], src)
            return tile

        def load_scales(src, width, name):
            tile = keep.tile([P, width], U8, name=name, align_bytes=64)
            nc.vector.memset(tile[:].bitcast(I32), 0)
            nc.sync.dma_start(tile[0:P:8, :].bitcast(I32), src[0].bitcast(I32))
            return tile

        def load_words(src, width, name):
            tile = keep.tile([P, width], U32, name=name, tag=name, align_bytes=64)
            nc.sync.dma_start(tile[:].bitcast(I32), src[0].rearrange("p n t -> p (n t)").bitcast(I32))
            return tile

        def load_column(src, name):
            tile = keep.tile([P, PACK], F32, name=name)
            nc.sync.dma_start(tile[:], src.rearrange("(p t) o -> p (t o)", t=PACK))
            return tile

        def place_scale_rows(queue, plane, picked):
            for a in range(4):
                queue.dma_start(plane[a:P:32, :].bitcast(I32), picked[8 * a:P:32, :].bitcast(I32))

        offs_l = load_list(offs, "offs_l")
        x_bytes = load_scales(x_scales, T, "x_bytes")
        d_bytes = load_scales(d_scales, G, "d_bytes")
        ka_l = load_list(ka, "ka_l")
        kb_l = load_list(kb, "kb_l")
        d_codes = load_words(d_words, G, "d_codes")
        x_codes = load_words(x_words, T, "x_codes")

        warm = keep.tile([P, 16], F32)
        nc.gpsimd.memset(warm[:, 0:1], 0.0)
        nc.scalar.activation(warm[:, 8:9], warm[:, 0:1], ACT.Sigmoid)

        plane1 = keep.tile([P, 2 * H + S], U8, align_bytes=64)
        nc.vector.memset(plane1[:].bitcast(I32), 0)
        hz_plane = keep.tile([P, S], U8, align_bytes=64)
        nc.vector.memset(hz_plane[:].bitcast(I32), 0)
        h2 = [keep.tile([P, S + SPARE], F32, name=f"h2_{b}") for b in range(4)]
        for b in range(4):
            nc.vector.memset(h2[b][:, S:], 0.0)

        picked1 = keep.tile([P, 2 * H + S], U8, tag="early", align_bytes=64)
        nc.vector.tensor_copy(picked1[:, 2 * H:], x_bytes[:].indirect(offs_l[:]))
        nc.vector.tensor_copy(picked1[:, 0:H], d_bytes[:].indirect(ka_l[:]))
        nc.vector.tensor_copy(picked1[:, H:2 * H], d_bytes[:].indirect(kb_l[:]))
        place_scale_rows(nc.scalar, plane1, picked1)

        dq = keep.tile([P, 2, H], U32, align_bytes=64)
        nc.vector.tensor_copy(dq[:, 0, :], d_codes[:].indirect(ka_l[:]))
        nc.vector.tensor_copy(dq[:, 1, :], d_codes[:].indirect(kb_l[:]))
        xq = keep.tile([P, S], U32, align_bytes=64)
        nc.vector.tensor_copy(xq[:], x_codes[:].indirect(offs_l[:]))

        def load_w(half, tag):
            tile = keep.tile([P, 2, PACK, N // 2], F32, name=f"w_raw_{half}", tag=tag, align_bytes=64)
            for i, src in ((1, w2), (0, w1)):
                rows = src.rearrange("(p j) m -> p j m", j=PACK)
                nc.sync.dma_start(tile[:, i], rows[:, :, half * 256:(half + 1) * 256])
            return tile

        n1_l = load_list(n1, "n1_l")
        n2_l = load_list(n2, "n2_l")
        n3_l = load_list(n3, "n3_l")
        n4_l = load_list(n4, "n4_l")
        hz_l = load_list(hz, "hz_l")
        n5_l = load_list(n5, "n5_l")
        sl_c = load_column(sl, "sl_c")
        w_raw = [load_w(0, "early")]
        th_c = load_column(th, "th_c")
        gn_c = load_column(gn, "gn_c")
        n8_l = load_list(n8, "n8_l")
        n9_l = load_list(n9, "n9_l")
        n6_l = load_list(n6, "n6_l")
        n7_l = load_list(n7, "n7_l")
        w_raw.append(load_w(1, "d_codes"))

        bias = keep.tile([P, PACK], F32)
        nc.vector.scalar_tensor_tensor(bias[:], sl_c[:], -1.0, th_c[:], ALU.mult, ALU.mult)

        h = [keep.tile([P, S], F32, name=f"h_{t}", tag=f"h_{t}") for t in range(4)]
        pab = [keep.tile([P, 2, W], F32, name=f"pab_{t}", tag=f"pab_{t}", align_bytes=64) for t in range(4)]
        ra = [keep.tile([P, W], F32, name=f"ra_{t}") for t in range(4)]
        ub = [keep.tile([P, S], F32, name=f"ub_{t}") for t in range(4)]
        sg = [keep.tile([P, S], F32, name=f"sg_{t}") for t in range(4)]
        z_rows = keep.tile([P, PACK, S], BF16, align_bytes=64)
        h_acc = {}

        def first_product(t):
            codes = keep.tile([P, 2, P], U32, name=f"d_dealt_{t}", tag="d_dealt", bufs=2, align_bytes=64)
            scales = keep.tile([P, 2, P], U8, name=f"d_dealt_s_{t}", align_bytes=64)
            nc.vector.tensor_copy(
                scales[:], plane1[:, 0:2 * H].rearrange("p (l m t) -> p l m t", l=2, t=PACK)[:, :, :, t]
            )
            nc.vector.tensor_copy(codes[:], dq[:].rearrange("p l (m t) -> p l m t", t=PACK)[:, :, :, t])
            h_acc[t] = psum.tile([P, S], F32, name=f"h_acc_{t}", tag=f"bank_{t}")
            for l in range(2):
                nc.tensor.matmul_mx(
                    out=h_acc[t][:], lhsT=codes[:, l, :].bitcast(FP8X4), lhsT_scale=scales[:, l, :],
                    rhs=xq[:].bitcast(FP8X4), rhs_scale=plane1[:, 2 * H:], start=(l == 0), stop=(l == 1),
                )

        def fetch_pairs(t):
            nc.vector.tensor_scalar(h[t][:], h_acc[t][:], 0.0625, None, ALU.mult)
            nc.scalar.activation(pab[t][:, 0, :], h[t][:].indirect(n1_l[:]), ACT.Copy)
            nc.scalar.activation(pab[t][:, 1, :], h[t][:].indirect(n2_l[:]), ACT.Copy)

        def put_larger(t):
            nc.vector.tensor_tensor(ra[t][:], pab[t][:, 0, :], pab[t][:, 1, :], ALU.max)
            nc.scalar.activation(ub[t][:].indirect(n3_l[:]), ra[t][:], ACT.Copy)

        def put_smaller(t):
            rb = keep.tile([P, W], F32, name=f"rb_{t}", tag=f"h_{(t + 2) % 4}")
            nc.vector.tensor_tensor(rb[:], pab[t][:, 0, :], pab[t][:, 1, :], ALU.min)
            nc.scalar.activation(ub[t][:].indirect(n4_l[:]), rb[:], ACT.Copy)

        def gate(t, c):
            cols = slice(c * HALF, (c + 1) * HALF)
            nc.scalar.activation(
                sg[t][:, cols], ub[t][:].indirect(n5_l[:, c * 8:(c + 1) * 8]), ACT.Sigmoid,
                bias=bias[:, t:t + 1], scale=sl_c[:, t:t + 1],
            )
            nc.vector.scalar_tensor_tensor(
                z_rows[:, t, cols], ub[t][:, cols], gn_c[:, t:t + 1], sg[t][:, cols], ALU.mult, ALU.mult
            )

        z_codes = keep.tile([P, S], U32, align_bytes=64)
        z_scales = keep.tile([P, S], U8, align_bytes=64)

        def quantise_z(c):
            cols = slice(c * HALF, (c + 1) * HALF)
            grouped = keep.tile([P, HALF, PACK], BF16, name=f"z_grouped_{c}", align_bytes=64)
            nc.vector.tensor_copy(
                grouped[:].rearrange("p (c i) t -> p c t i", i=4),
                z_rows[:, :, cols].rearrange("p t (c i) -> p c t i", i=4),
            )
            nc.vector.quantize_mx(
                out=z_codes[:, cols].bitcast(FP8X4), scales=z_scales[:, cols],
                in_=grouped[:].rearrange("p c t -> p (c t)"),
            )

        w_codes = [keep.tile([P, 2, P], U32, name=f"w_codes_{b}", align_bytes=64) for b in range(4)]
        w_scales = [keep.tile([P, 2, P], U8, name=f"w_scales_{b}", align_bytes=64) for b in range(4)]
        w_grouped = {}

        def group_w(b, tag):
            w_grouped[b] = keep.tile([P, 2, P, PACK], BF16, name=f"w_grouped_{b}", tag=tag, align_bytes=64)
            for i in range(2):
                nc.vector.tensor_copy(
                    w_grouped[b][:, i].rearrange("p (c i) t -> p c t i", i=4),
                    w_raw[b // 2][:, i, :, (b % 2) * P:(b % 2 + 1) * P].rearrange("p t (c i) -> p c t i", i=4),
                )

        def quantise_w(b):
            nc.vector.quantize_mx(
                out=w_codes[b][:].rearrange("p i m -> p (i m)").bitcast(FP8X4),
                scales=w_scales[b][:].rearrange("p i m -> p (i m)"),
                in_=w_grouped[b][:].rearrange("p i m t -> p (i m t)"),
            )

        first_product(0)
        first_product(1)
        fetch_pairs(0)
        first_product(2)
        fetch_pairs(1)
        first_product(3)
        put_larger(0)
        fetch_pairs(2)
        fetch_pairs(3)
        put_larger(1)
        put_larger(2)
        put_smaller(0)
        put_larger(3)
        put_smaller(1)

        put_smaller(2)
        put_smaller(3)

        picked_hz = keep.tile([P, S], U8, tag="pab_2", align_bytes=64)
        nc.vector.tensor_copy(picked_hz[:], x_bytes[:].indirect(hz_l[:]))
        place_scale_rows(nc.sync, hz_plane, picked_hz)
        x_hz = keep.tile([P, S], U32, tag="pab_3", align_bytes=64)
        nc.vector.tensor_copy(x_hz[:], x_codes[:].indirect(hz_l[:]))

        group_w(0, "wg0")
        group_w(1, "wg1")
        quantise_w(0)
        quantise_w(1)
        for c in range(2):
            for t in range(4):
                gate(t, c)
            quantise_z(c)

        g89 = [keep.tile([P, 2, S], F32, name=f"g89_{b}", tag=f"g89_{b}", align_bytes=64) for b in range(4)]
        updn = [keep.tile([P, 2, S], F32, name=f"updn_{b}") for b in range(4)]
        page = [keep.tile([P, U], F32, name=f"page_{b}") for b in range(4)]

        def second_product(b, c):
            cols = slice(c * HALF, (c + 1) * HALF)
            acc = psum.tile([P, HALF], F32, name=f"h2_acc_{b}_{c}", tag=f"bank_{4 * c + b}")
            nc.tensor.matmul_mx(
                out=acc[:], lhsT=w_codes[b][:, 1, :].bitcast(FP8X4), lhsT_scale=w_scales[b][:, 1, :],
                rhs=x_hz[:, cols].bitcast(FP8X4), rhs_scale=hz_plane[:, cols], start=True, stop=False,
            )
            nc.tensor.matmul_mx(
                out=acc[:], lhsT=w_codes[b][:, 0, :].bitcast(FP8X4), lhsT_scale=w_scales[b][:, 0, :],
                rhs=z_codes[:, cols].bitcast(FP8X4), rhs_scale=z_scales[:, cols], start=False, stop=True,
            )
            nc.vector.tensor_copy(h2[b][:, cols], acc[:])

        def fetch_neighbours(b):
            nc.scalar.activation(g89[b][:, 0, :], h2[b][:].indirect(n8_l[:]), ACT.Copy)
            nc.scalar.activation(g89[b][:, 1, :], h2[b][:].indirect(n9_l[:]), ACT.Copy)
            nc.vector.tensor_tensor(updn[b][:, 0, :], h2[b][:, 0:S], g89[b][:, 0, :], ALU.max)
            nc.vector.tensor_tensor(updn[b][:, 1, :], h2[b][:, 0:S], g89[b][:, 1, :], ALU.subtract)

        def put_page(b):
            nc.scalar.activation(page[b][:].indirect(n6_l[:]), updn[b][:, 0, :], ACT.Copy)
            nc.scalar.activation(page[b][:].indirect(n7_l[:]), updn[b][:, 1, :], ACT.Copy)
            nc.sync.dma_start(out[b * P:(b + 1) * P, :], page[b][:])

        second_product(0, 0)
        second_product(0, 1)
        second_product(1, 0)
        second_product(1, 1)
        fetch_neighbours(0)
        fetch_neighbours(1)
        group_w(2, "g89_0")
        quantise_w(2)
        second_product(2, 0)
        second_product(2, 1)
        put_page(0)
        group_w(3, "g89_1")
        quantise_w(3)
        second_product(3, 0)
        second_product(3, 1)
        fetch_neighbours(2)
        put_page(1)
        fetch_neighbours(3)
        put_page(2)
        put_page(3)
